import numpy as np
import ml_dtypes


def mxq(x, axis, fmt="e4m3"):
    dtype, down = {"e4m3": (ml_dtypes.float8_e4m3fn, 7), "e5m2": (ml_dtypes.float8_e5m2, 14)}[fmt]
    v = np.moveaxis(np.asarray(x, np.float32).astype(ml_dtypes.bfloat16).astype(np.float64), axis, -1)
    blocks = v.reshape(v.shape[:-1] + (-1, 32))
    amax = np.abs(blocks).max(-1, keepdims=True)
    byte = np.maximum(np.where(amax > 0, np.frexp(amax)[1] - 1 + 127, 0) - down, 1)
    scale = np.exp2(byte - 127.0)
    codes = (blocks / scale).astype(np.float32).astype(dtype).astype(np.float64)
    return np.moveaxis((codes * scale).reshape(v.shape), -1, axis)


WIDE = False


def mx_kscale(k):
    if not WIDE:
        return np.ones(k)
    levels = np.array([10, -10, 5, -5, 0])
    if k % 512:
        return np.exp2(np.random.permutation(np.resize(levels, k // 32))).repeat(32)
    a = np.empty((k // 512, 16))
    for p in range(k // 512):
        a[p, :8] = np.random.permutation(np.resize(levels, 8))
        for g in range(8):
            far = levels[np.abs(levels - a[p, g]) >= 10]
            a[p, g + 8] = far[np.random.randint(len(far))]
    return np.exp2(a.ravel()).repeat(32)


def f64(x):
    return np.asarray(x).astype(np.float64)


def striped(idx):
    return np.tile(idx.reshape(-1, 16).T, (8, 1)).astype(np.uint16)


def unstriped(offs):
    return offs[:16].T.reshape(-1).astype(np.int64)


E2M1 = np.array([0.0, 0.5, 1.0, 1.5, 2.0, 3.0, 4.0, 6.0, -0.0, -0.5, -1.0, -1.5, -2.0, -3.0, -4.0, -6.0])


def pack_weight(w, fmt):
    k, n = w.shape
    w = f64(np.asarray(w, np.float32).astype(ml_dtypes.bfloat16)).reshape(k // 32, 32, n)
    amax = np.abs(w).max(1)
    if fmt == "e4m3":
        byte = np.frexp(amax)[1] - 1 + 127 - 7
    else:
        mant, ex = np.frexp(amax / 6.0)
        byte = np.where(mant > 0.5, ex, ex - 1) + 127
    byte = np.clip(np.where(amax > 0, byte, 1), 1, 254)
    scaled = (w * np.exp2(127.0 - byte)[:, None, :]).reshape(k, n).astype(np.float32)
    by_word = np.ascontiguousarray(scaled.reshape(k // 512, 128, 4, n).transpose(0, 1, 3, 2))
    if fmt == "e4m3":
        words = by_word.astype(ml_dtypes.float8_e4m3fn).view(np.uint8)
    else:
        c = by_word.astype(ml_dtypes.float4_e2m1fn).view(np.uint8) & 0xF
        words = (c[..., 0::2] | (c[..., 1::2] << 4)).reshape(k // 512, 128, 2 * n)
    return np.ascontiguousarray(words), np.ascontiguousarray(byte.astype(np.uint8).reshape(k // 512, 16, n))


def unpack_weight(words, scales, fmt):
    g, _, n = scales.shape
    words = np.ascontiguousarray(words).reshape(g, 128, n, -1)
    if fmt == "e4m3":
        vals = words.view(ml_dtypes.float8_e4m3fn).astype(np.float64)
    else:
        nib = np.empty((g, 128, n, 4), np.uint8)
        nib[..., 0::2] = words & 0xF
        nib[..., 1::2] = words >> 4
        vals = E2M1[nib]
    vals = vals * np.repeat(np.exp2(scales.astype(np.float64) - 127.0), 8, axis=1)[..., None]
    return vals.transpose(0, 1, 3, 2).reshape(g * 512, n)


def gelu(v):
    return 0.5 * v * (1.0 + np.tanh(np.sqrt(2.0 / np.pi) * (v + 0.044715 * v**3)))


def often(T, S):
    return np.random.permutation(T)[(T * np.random.uniform(0, 1, S) ** 4).astype(np.int64)]


def bf(x):
    return np.asarray(x, np.float32).astype(ml_dtypes.bfloat16)


def planes(Y):
    n, m = Y.shape
    b = f64(bf(Y)).reshape(n // 32, 32, m)
    amax = np.abs(b).max(1)
    byte = np.clip(np.where(amax > 0, np.frexp(amax)[1] - 1 + 127 - 7, 1), 1, 254)
    codes = (b * np.exp2(127.0 - byte)[:, None, :]).reshape(n, m).astype(np.float32).astype(ml_dtypes.float8_e4m3fn).view(np.uint8)
    words = codes.reshape(n // 512, 128, 4, m).transpose(0, 1, 3, 2)
    return np.ascontiguousarray(words), np.ascontiguousarray(byte.astype(np.uint8).reshape(n // 512, 16, m))


T, S, P, K, K2, H, N = 4096, 1024, 512, 1024, 512, 1024, 1024

def setup_inputs():
    n = np.random.standard_normal
    s = mx_kscale(K)[:, None]
    s2 = mx_kscale(K2)[:, None]
    u = mx_kscale(H)[:, None]
    d = {}
    d["tab_words"], d["tab_scales"] = pack_weight(n((K, T)) * s, "e4m3")
    d["tab2_words"], d["tab2_scales"] = pack_weight(n((K2, T)) * s2, "e4m3")
    d["tab3_words"], d["tab3_scales"] = pack_weight(n((K2, T)) * s2, "e4m3")
    d["offs"] = striped(np.random.permutation(T)[:S])
    d["offs2"] = striped(np.random.permutation(T)[:S])
    d["offs3"] = striped(np.random.permutation(T)[:S])
    d["pos1"] = striped(np.random.permutation(S)[:P])
    d["pos2"] = striped(often(S, P))
    d["pos3"] = striped(often(S, P))
    d["wa"] = (1.5 * n((K, H)) / K ** 0.5 / s).astype(np.float32)
    d["w4_words"], d["w4_scales"] = pack_weight(1.3 * n((K2, H)) / K2 ** 0.5 / s2, "e2m1")
    d["w8_words"], d["w8_scales"] = pack_weight(1.2 * n((K2, H)) / K2 ** 0.5 / s2, "e4m3")
    d["gain"] = (np.exp(0.3 * n(H)) * u[:, 0]).astype(np.float32)
    d["wo"] = (n((H, N)) * np.exp(0.8 * n(N)) / H ** 0.5 / u).astype(np.float32)
    return d

def reference(tab_words, tab_scales, tab2_words, tab2_scales, tab3_words, tab3_scales, offs, offs2, offs3,
              pos1, pos2, pos3, wa, w4_words, w4_scales, w8_words, w8_scales, gain, wo):
    v = unpack_weight(tab_words, tab_scales, "e4m3")[:, unstriped(offs)]
    v2 = unpack_weight(tab2_words, tab2_scales, "e4m3")[:, unstriped(offs2)]
    v3 = unpack_weight(tab3_words, tab3_scales, "e4m3")[:, unstriped(offs3)]
    a = mxq(f64(wa), 0, "e4m3").T @ v
    b = unpack_weight(w4_words, w4_scales, "e2m1").T @ v2
    d = unpack_weight(w8_words, w8_scales, "e4m3").T @ v3
    e = b[:, unstriped(pos2)] - d[:, unstriped(pos3)]
    usable = e / (1.0 + np.exp(-e))
    f = a[:, unstriped(pos1)] - usable
    z = f64(gain)[:, None] * (f / (1.0 + np.exp(-f)))
    y = mxq(f64(wo), 0, "e4m3").T @ mxq(z, 0, "e4m3")
    words, scales = planes(y)
    return y, words, scales

@@ -1,0 +1,338 @@
+from contextlib import ExitStack
+
+import concourse.mybir as mybir
+
+T, S, NP, K, K2, H, N = 4096, 1024, 512, 1024, 512, 1024, 1024
+FLOPS = 2 * (K * H * S + 2 * K2 * H * S + H * N * NP)
+
+F32 = mybir.dt.float32
+BF16 = mybir.dt.bfloat16
+I32 = mybir.dt.int32
+U32 = mybir.dt.uint32
+U16 = mybir.dt.uint16
+U8 = mybir.dt.uint8
+FP8X4 = mybir.dt.float8_e4m3fn_x4
+FP4X4 = mybir.dt.float4_e2m1fn_x4
+SILU = mybir.ActivationFunctionType.Silu
+COPY = mybir.ActivationFunctionType.Copy
+SUB = mybir.AluOpType.subtract
+
+P = 128
+BANK = 512
+SLICES = H // P
+WINDOW_BYTES = 4 * T
+DB = 3
+BB = 4
+LAG = 3
+AB = 2
+PARTS = 2
+YB = 3
+ROW3 = 4
+ROW1 = 8
+
+
+def tile_list_sprinkler_layout_review_kernel(
+    tc, tab_words, tab_scales, tab2_words, tab2_scales, tab3_words, tab3_scales, offs, offs2, offs3,
+    pos1, pos2, pos3, wa, w4_words, w4_scales, w8_words, w8_scales, gain, wo, out_0, out_1, out_2,
+):
+    nc = tc.nc
+    with ExitStack() as ctx:
+        keep = ctx.enter_context(tc.tile_pool(name="keep", bufs=1))
+        work = ctx.enter_context(tc.tile_pool(name="work", bufs=1))
+        arena = ctx.enter_context(tc.tile_pool(name="arena", bufs=1))
+        psum = ctx.enter_context(tc.psum_pool(name="psum", bufs=8))
+
+        def load_list(src, name):
+            tile = keep.tile([P, src.shape[1]], U16, name=name)
+            nc.sync.dma_start(tile[:], src)
+            return tile
+
+        def words_window(name, place):
+            return arena.tile([P, T], U32, name=name, offset=place * WINDOW_BYTES)
+
+        def load_words(tile, src, part, parts):
+            cols = slice(part * T // parts, (part + 1) * T // parts)
+            nc.sync.dma_start(tile[:, cols].bitcast(I32), src[:, cols, :].rearrange("p n t -> p (n t)").bitcast(I32))
+
+        def load_scale_rows(tile, src, q, row, queue):
+            passes = src.shape[0]
+            rows = src[:, 4 * q : 4 * q + 4, :] if passes > 1 else src[0, 4 * q : 4 * q + 4, :]
+            queue.dma_start(tile[32 * q + row : 32 * q + row + 4 * passes, :].bitcast(I32), rows.bitcast(I32))
+
+        def gather_bytes(window, offsets, dtype, name):
+            tile = keep.tile([P, S], dtype, name=name, align_bytes=64)
+            nc.vector.tensor_copy(tile[:], window[:].indirect(offsets[:]))
+            return tile
+
+        def deal(raw, name):
+            width = raw.shape[1]
+            tile = keep.tile([P, width], U8, name=name, align_bytes=64)
+            nc.vector.tensor_copy(
+                tile[:].bitcast(I32).rearrange("p (b t g i) -> p b t g i", b=2, t=4, g=16),
+                raw[:].bitcast(I32).rearrange("p (b g t i) -> p b t g i", b=2, t=4, g=16),
+            )
+            return tile
+
+        def quantize(grouped, name):
+            codes = keep.tile([P, BANK], U32, name=name + "_codes", align_bytes=64)
+            scales = keep.tile([P, BANK], U8, name=name + "_scales", align_bytes=64)
+            nc.vector.quantize_mx(out=codes[:].bitcast(FP8X4), scales=scales[:], in_=grouped[:])
+            return codes, scales
+
+        def grouped_tile(name):
+            return work.tile([P, 4 * BANK], BF16, name=name, tag="grouped", bufs=3, align_bytes=64)
+
+        def cast(on_scalar, out, in_):
+            if on_scalar:
+                nc.scalar.copy(out, in_)
+            else:
+                nc.vector.tensor_copy(out, in_)
+
+        def scale_window(name):
+            return work.tile([P, T], U8, name=name, tag="page", bufs=3, align_bytes=64)
+
+        sc2_win = scale_window("sc2_win")
+        sc3_win = scale_window("sc3_win")
+        sc1_win = scale_window("sc1_win")
+        w4s_raw = keep.tile([P, H], U8, name="w4s_raw", align_bytes=64)
+        w8s_raw = keep.tile([P, H], U8, name="w8s_raw", align_bytes=64)
+        for plane in (sc2_win, sc3_win, sc1_win, w4s_raw, w8s_raw):
+            nc.vector.memset(plane[:].bitcast(I32), 0)
+        warm = keep.tile([P, 8], F32, name="warm")
+        nc.vector.memset(warm[:], 0.0)
+        nc.scalar.activation(warm[:, 1:2], warm[:, 0:1], SILU)
+
+        tab2_win = words_window("tab2_win", 0)
+        tab3_win = words_window("tab3_win", 1)
+        offs2_t = load_list(offs2, "offs2_t")
+        offs3_t = load_list(offs3, "offs3_t")
+        for q in range(4):
+            load_scale_rows(sc2_win, tab2_scales, q, 0, nc.sync)
+        load_words(tab2_win, tab2_words[0], 0, 2)
+        load_words(tab2_win, tab2_words[0], 1, 2)
+        w4_raw = keep.tile([P, 2 * H], U8, name="w4_raw", align_bytes=64)
+        nc.sync.dma_start(w4_raw[:].bitcast(I32), w4_words[0].bitcast(I32))
+        for q in range(4):
+            load_scale_rows(w4s_raw, w4_scales, q, 0, nc.sync)
+        load_words(tab3_win, tab3_words[0], 0, 2)
+        for q in range(4):
+            load_scale_rows(sc3_win, tab3_scales, q, ROW3, nc.sync)
+        load_words(tab3_win, tab3_words[0], 1, 2)
+        w8_raw = keep.tile([P, 4 * H], U8, name="w8_raw", align_bytes=64)
+        nc.sync.dma_start(w8_raw[:].bitcast(I32), w8_words[0].rearrange("p n t -> p (n t)").bitcast(I32))
+        for q in range(4):
+            load_scale_rows(w8s_raw, w8_scales, q, ROW3, nc.sync)
+        offs_t = load_list(offs, "offs_t")
+        pos3_t = load_list(pos3, "pos3_t")
+        pos2_t = load_list(pos2, "pos2_t")
+
+        for q in range(4):
+            load_scale_rows(sc1_win, tab_scales, q, ROW1, nc.gpsimd)
+
+        v2s = gather_bytes(sc2_win, offs2_t, U8, "v2s")
+        v3s = gather_bytes(sc3_win, offs3_t, U8, "v3s")
+        v2w = gather_bytes(tab2_win, offs2_t, U32, "v2w")
+        w4_d = deal(w4_raw, "w4_d")
+        w4s_d = deal(w4s_raw, "w4s_d")
+
+        def first_stage(passes, tag, bufs, name):
+            window = work.tile([P, S], F32, name=name, tag=tag, bufs=bufs)
+            for h in range(S // BANK):
+                cols = slice(h * BANK, (h + 1) * BANK)
+                acc = psum.tile([P, BANK], F32, name="acc", tag="acc")
+                for n, (lw, ls, rw, rs, row) in enumerate(passes):
+                    nc.tensor.matmul_mx(
+                        out=acc[:], lhsT=lw, lhsT_scale=ls, rhs=rw[:, cols].bitcast(FP8X4), rhs_scale=rs[row:P, cols],
+                        start=(n == 0), stop=(n == len(passes) - 1),
+                    )
+                nc.scalar.copy(window[:, cols], acc[:])
+            return window
+
+        def stage_b(s):
+            return first_stage(
+                [(w4_d[:, 256 * s : 256 * s + 256].bitcast(FP4X4), w4s_d[:, P * s : P * s + P], v2w, v2s, 0)],
+                "rows", 8, "b_win")
+
+        def stage_d(s):
+            return first_stage(
+                [(w8_d[:, 512 * s : 512 * s + 512].bitcast(FP8X4), w8s_d[ROW3:P, P * s : P * s + P], v3w, v3s, ROW3)],
+                "d_rows", DB, "d_win")
+
+        b_win = {s: stage_b(s) for s in range(BB)}
+
+        w8_d = deal(w8_raw, "w8_d")
+        w8s_d = deal(w8s_raw, "w8s_d")
+        v3w = gather_bytes(tab3_win, offs3_t, U32, "v3w")
+        v1s = gather_bytes(sc1_win, offs_t, U8, "v1s")
+
+        wa_raw = {}
+
+        def load_wa(b):
+            for a in range(2):
+                raw = arena.tile([P, 4, BANK], F32, name="wa_raw%d%d" % (a, b), offset=(2 * b + a) * WINDOW_BYTES // 2)
+                nc.sync.dma_start(
+                    raw[:], wa[512 * a : 512 * a + 512, 512 * b : 512 * b + 512].rearrange("(p j) c -> p j c", j=4)
+                )
+                wa_raw[a, b] = raw
+
+        load_wa(0)
+
+        tab_win = [words_window("tab_win%d" % a, 2 + a) for a in range(2)]
+        for a in range(2):
+            load_words(tab_win[a], tab_words[a], 0, 1)
+        load_wa(1)
+        pos1_t = load_list(pos1, "pos1_t")
+
+        def cast_wa(a, b):
+            grouped = grouped_tile("wa_grouped")
+            cast(True,
+                 grouped[:].rearrange("p (t g i j) -> p g t i j", t=4, g=16, i=8),
+                 wa_raw[a, b][:].rearrange("p j (g t i) -> p g t i j", t=4, i=8))
+            return grouped
+
+        def cast_wo(b, g, on_scalar):
+            grouped = grouped_tile("wo_grouped")
+            cast(on_scalar,
+                 grouped[:].rearrange("p (t m j) -> p m t j", t=4, j=4),
+                 wo_raw[b][:, :, 512 * g : 512 * g + 512].rearrange("p j (m t) -> p m t j", t=4))
+            return grouped
+
+        def pick_d(d_win):
+            picked = work.tile([P, NP], F32, name="d_picked", tag="tmp", bufs=4)
+            nc.vector.tensor_copy(picked[:], d_win[:].indirect(pos3_t[:]))
+            return picked
+
+        usable = {}
+        wa_q = {}
+        wa_grouped = {}
+        v1w = {}
+        d_win = {s: stage_d(s) for s in range(DB)}
+        d_picked = {0: pick_d(d_win[0])}
+        for s in range(SLICES + LAG):
+            if s + 1 < SLICES:
+                d_picked[s + 1] = pick_d(d_win[s + 1])
+            if s < SLICES:
+                usable[s] = keep.tile([P, NP], F32, name="usable%d" % s)
+                nc.vector.tensor_tensor(usable[s][:], b_win[s][:].indirect(pos2_t[:]), d_picked[s][:], SUB)
+            if s + DB < SLICES:
+                d_win[s + DB] = stage_d(s + DB)
+            if s + BB < SLICES:
+                b_win[s + BB] = stage_b(s + BB)
+            if s < SLICES:
+                piece = (s // 2 % 2, s // 4)
+                if s % 2 == 0:
+                    wa_grouped[piece] = cast_wa(*piece)
+                else:
+                    wa_q[piece] = quantize(wa_grouped[piece], "wa%d%d" % piece)
+            if s >= LAG:
+                nc.scalar.activation(usable[s - LAG][:], usable[s - LAG][:], SILU)
+            if s in (4, 6):
+                a = len(v1w)
+                v1w[a] = gather_bytes(tab_win[a], offs_t, U32, "v1w%d" % a)
+
+        wo_raw = []
+        gain_t = keep.tile([P, SLICES, 8], F32, name="gain_t")
+        gain_v = gain.rearrange("(b g t i o) -> b t g i o", b=2, g=16, t=4, i=8)
+        for b in range(2):
+            raw = arena.tile([P, 4, N], F32, name="wo_raw%d" % b, offset=(2 + b) * WINDOW_BYTES)
+            rows = wo[512 * b : 512 * b + 512, :].rearrange("(g t i) n -> t g i n", t=4, i=8)
+            for t in range(4):
+                nc.sync.dma_start(raw[:, t, :], rows[t])
+                with nc.allow_non_contiguous_dma(reason="one gain value for each partition"):
+                    nc.sync.dma_start(gain_t[:, 4 * b + t, 0:1], gain_v[b, t])
+            wo_raw.append(raw)
+
+        def stage_a(s):
+            b, t = divmod(s, 4)
+            cols = slice(P * t, P * t + P)
+            return first_stage(
+                [(wa_q[a, b][0][:, cols].bitcast(FP8X4), wa_q[a, b][1][:, cols], v1w[a], v1s, ROW1 + 4 * a) for a in range(2)],
+                "rows", 8, "a_win")
+
+        def hazard(s, part, parts):
+            width = NP // parts
+            f = work.tile([P, width], F32, name="f", tag="tmp", bufs=4)
+            places = pos1_t[:, part * width // 16 : (part + 1) * width // 16]
+            nc.vector.tensor_tensor(f[:], a_win[s][:].indirect(places), usable[s][:, part * width : (part + 1) * width], SUB)
+            return f
+
+        def gained(s, f, z_rows):
+            nc.scalar.activation(f[:], f[:], SILU)
+            nc.scalar.activation(z_rows[:, s % 4, :], f[:], COPY, scale=gain_t[:, s, 0:1])
+
+        def weave(rows, name):
+            width = rows.shape[2]
+            grouped = work.tile([P, 4 * width], BF16, name=name, tag="grouped", bufs=3, align_bytes=64)
+            nc.vector.tensor_copy(grouped[:].rearrange("p (j t) -> p j t", t=4), rows[:].rearrange("p t j -> p j t"))
+            return grouped
+
+        wo_q = {}
+        wo_grouped = {}
+        a_win = {s: stage_a(s) for s in range(AB)}
+        z_rows = work.tile([P, 4, NP], BF16, name="z_rows", tag="page", bufs=3, align_bytes=64)
+        for s in range(4):
+            f = hazard(s, 0, 1)
+            for n in range(AB + 2 * s, min(SLICES, AB + 2 * s + 2)):
+                a_win[n] = stage_a(n)
+            piece = divmod(s, 2)
+            wo_grouped[piece] = cast_wo(piece[0], piece[1], s in (0,))
+            gained(s, f, z_rows)
+            wo_q[piece] = quantize(wo_grouped[piece], "wo%d%d" % piece)
+        z0_grouped = weave(z_rows, "z_grouped")
+
+        y_scales = keep.tile([P, 2, NP], U8, name="y_scales", align_bytes=64)
+        y_codes = [keep.tile([P, NP], U32, name="y_codes%d" % g, align_bytes=64) for g in range(2)]
+        z1_codes = keep.tile([P, NP], U32, name="z1_codes", align_bytes=64)
+        z1_scales = keep.tile([P, NP], U8, name="z1_scales", align_bytes=64)
+        width = NP // PARTS
+
+        def make_z1(part):
+            rows = work.tile([P, 4, width], BF16, name="z1_rows", tag="page", bufs=3, align_bytes=64)
+            for s in range(4, SLICES):
+                gained(s, hazard(s, part, PARTS), rows)
+            return rows
+
+        def last_stage(part, rows):
+            js = slice(part * width, (part + 1) * width)
+            grouped = weave(rows, "z_grouped")
+            nc.vector.quantize_mx(out=z1_codes[:, js].bitcast(FP8X4), scales=z1_scales[:, js], in_=grouped[:])
+            z_q = [z0_q, (z1_codes, z1_scales)]
+            y_rows = []
+            for g in range(2):
+                rows = work.tile([P, 4, width], F32, name="y_rows", tag="y_rows", bufs=YB)
+                for t in range(4):
+                    cols = slice(P * t, P * t + P)
+                    acc = psum.tile([P, width], F32, name="acc", tag="acc")
+                    for b in range(2):
+                        nc.tensor.matmul_mx(
+                            out=acc[:], lhsT=wo_q[b, g][0][:, cols].bitcast(FP8X4), lhsT_scale=wo_q[b, g][1][:, cols],
+                            rhs=z_q[b][0][:, js].bitcast(FP8X4), rhs_scale=z_q[b][1][:, js], start=(b == 0), stop=(b == 1),
+                        )
+                    nc.scalar.copy(rows[:, t, :], acc[:])
+                nc.sync.dma_start(out_0[512 * g : 512 * g + 512, js].rearrange("(p t) j -> p t j", t=4), rows[:])
+                y_rows.append(rows)
+            return y_rows
+
+        def planes(part, y_rows):
+            js = slice(part * width, (part + 1) * width)
+            for g in range(2):
+                grouped = weave(y_rows[g], "y_grouped")
+                nc.vector.quantize_mx(out=y_codes[g][:, js].bitcast(FP8X4), scales=y_scales[:, g, js], in_=grouped[:])
+                nc.sync.dma_start(
+                    out_1[g][:, js, :].rearrange("p m t -> p (m t)").bitcast(I32), y_codes[g][:, js].bitcast(I32))
+
+        z1_rows = {0: make_z1(0)}
+        z0_q = quantize(z0_grouped, "z0")
+        y_rows = {}
+        for part in range(PARTS):
+            if part + 1 < PARTS:
+                z1_rows[part + 1] = make_z1(part + 1)
+            y_rows[part] = last_stage(part, z1_rows[part])
+            if part > 0:
+                planes(part - 1, y_rows[part - 1])
+        planes(PARTS - 1, y_rows[PARTS - 1])
+        for q in range(4):
+            nc.sync.dma_start(
+                out_2[:, 4 * q : 4 * q + 4, :].rearrange("g q m -> q g m").bitcast(I32),
+                y_scales[32 * q : 32 * q + 4, :, :].bitcast(I32),
+            )

@@ -27,6 +27,9 @@ LAG = 3
 AB = 2
 PARTS = 2
 YB = 3
+TB = 5
+LEAD = 3
+RB = 7
 ROW3 = 4
 ROW1 = 8
 
@@ -68,8 +71,8 @@ def tile_list_sprinkler_layout_review_kernel(
             width = raw.shape[1]
             tile = keep.tile([P, width], U8, name=name, align_bytes=64)
             nc.vector.tensor_copy(
-                tile[:].bitcast(I32).rearrange("p (b t g i) -> p b t g i", b=2, t=4, g=16),
-                raw[:].bitcast(I32).rearrange("p (b g t i) -> p b t g i", b=2, t=4, g=16),
+                tile[:].bitcast(I32).rearrange("p (b t u i) -> p b u t i", b=2, t=4, u=32),
+                raw[:].bitcast(I32).rearrange("p (b u t i) -> p b u t i", b=2, t=4, u=32),
             )
             return tile
 
@@ -122,9 +125,9 @@ def tile_list_sprinkler_layout_review_kernel(
         nc.sync.dma_start(w8_raw[:].bitcast(I32), w8_words[0].rearrange("p n t -> p (n t)").bitcast(I32))
         for q in range(4):
             load_scale_rows(w8s_raw, w8_scales, q, ROW3, nc.sync)
-        offs_t = load_list(offs, "offs_t")
-        pos3_t = load_list(pos3, "pos3_t")
         pos2_t = load_list(pos2, "pos2_t")
+        pos3_t = load_list(pos3, "pos3_t")
+        offs_t = load_list(offs, "offs_t")
 
         for q in range(4):
             load_scale_rows(sc1_win, tab_scales, q, ROW1, nc.gpsimd)
@@ -151,7 +154,7 @@ def tile_list_sprinkler_layout_review_kernel(
         def stage_b(s):
             return first_stage(
                 [(w4_d[:, 256 * s : 256 * s + 256].bitcast(FP4X4), w4s_d[:, P * s : P * s + P], v2w, v2s, 0)],
-                "rows", 8, "b_win")
+                "rows", RB, "b_win")
 
         def stage_d(s):
             return first_stage(
@@ -163,7 +166,6 @@ def tile_list_sprinkler_layout_review_kernel(
         w8_d = deal(w8_raw, "w8_d")
         w8s_d = deal(w8s_raw, "w8s_d")
         v3w = gather_bytes(tab3_win, offs3_t, U32, "v3w")
-        v1s = gather_bytes(sc1_win, offs_t, U8, "v1s")
 
         wa_raw = {}
 
@@ -186,38 +188,36 @@ def tile_list_sprinkler_layout_review_kernel(
         def cast_wa(a, b):
             grouped = grouped_tile("wa_grouped")
             cast(True,
-                 grouped[:].rearrange("p (t g i j) -> p g t i j", t=4, g=16, i=8),
-                 wa_raw[a, b][:].rearrange("p j (g t i) -> p g t i j", t=4, i=8))
+                 grouped[:].rearrange("p (t u i j) -> p u t j i", t=4, i=4, j=4),
+                 wa_raw[a, b][:].rearrange("p j (u t i) -> p u t j i", t=4, i=4))
             return grouped
 
         def cast_wo(b, g, on_scalar):
             grouped = grouped_tile("wo_grouped")
             cast(on_scalar,
-                 grouped[:].rearrange("p (t m j) -> p m t j", t=4, j=4),
-                 wo_raw[b][:, :, 512 * g : 512 * g + 512].rearrange("p j (m t) -> p m t j", t=4))
+                 grouped[:].rearrange("p (t m j) -> p m j t", t=4, j=4),
+                 wo_raw[b][:, :, 512 * g : 512 * g + 512].rearrange("p j (m t) -> p m j t", t=4))
             return grouped
 
-        def pick_d(d_win):
-            picked = work.tile([P, NP], F32, name="d_picked", tag="tmp", bufs=4)
-            nc.vector.tensor_copy(picked[:], d_win[:].indirect(pos3_t[:]))
+        def pick_b(s):
+            picked = work.tile([P, NP], F32, name="b_picked", tag="tmp", bufs=TB)
+            nc.vector.tensor_copy(picked[:], b_win[s][:].indirect(pos2_t[:]))
             return picked
 
         usable = {}
         wa_q = {}
         wa_grouped = {}
         v1w = {}
-        d_win = {s: stage_d(s) for s in range(DB)}
-        d_picked = {0: pick_d(d_win[0])}
+        b_picked = {s: pick_b(s) for s in range(BB)}
+        v1s = gather_bytes(sc1_win, offs_t, U8, "v1s")
         for s in range(SLICES + LAG):
-            if s + 1 < SLICES:
-                d_picked[s + 1] = pick_d(d_win[s + 1])
             if s < SLICES:
+                d_win = stage_d(s)
                 usable[s] = keep.tile([P, NP], F32, name="usable%d" % s)
-                nc.vector.tensor_tensor(usable[s][:], b_win[s][:].indirect(pos2_t[:]), d_picked[s][:], SUB)
-            if s + DB < SLICES:
-                d_win[s + DB] = stage_d(s + DB)
-            if s + BB < SLICES:
-                b_win[s + BB] = stage_b(s + BB)
+                nc.vector.tensor_tensor(usable[s][:], d_win[:].indirect(pos3_t[:]), b_picked[s][:], SUB)
+            if BB <= s + LEAD < SLICES:
+                b_win[s + LEAD] = stage_b(s + LEAD)
+                b_picked[s + LEAD] = pick_b(s + LEAD)
             if s < SLICES:
                 piece = (s // 2 % 2, s // 4)
                 if s % 2 == 0:
@@ -225,17 +225,17 @@ def tile_list_sprinkler_layout_review_kernel(
                 else:
                     wa_q[piece] = quantize(wa_grouped[piece], "wa%d%d" % piece)
             if s >= LAG:
-                nc.scalar.activation(usable[s - LAG][:], usable[s - LAG][:], SILU)
+                nc.scalar.activation(usable[s - LAG][:], usable[s - LAG][:], SILU, scale=-1.0)
             if s in (4, 6):
                 a = len(v1w)
                 v1w[a] = gather_bytes(tab_win[a], offs_t, U32, "v1w%d" % a)
 
         wo_raw = []
         gain_t = keep.tile([P, SLICES, 8], F32, name="gain_t")
-        gain_v = gain.rearrange("(b g t i o) -> b t g i o", b=2, g=16, t=4, i=8)
+        gain_v = gain.rearrange("(b u t i o) -> b t u i o", b=2, u=32, t=4, i=4)
         for b in range(2):
             raw = arena.tile([P, 4, N], F32, name="wo_raw%d" % b, offset=(2 + b) * WINDOW_BYTES)
-            rows = wo[512 * b : 512 * b + 512, :].rearrange("(g t i) n -> t g i n", t=4, i=8)
+            rows = wo[512 * b : 512 * b + 512, :].rearrange("(u t i) n -> t u i n", t=4, i=4)
             for t in range(4):
                 nc.sync.dma_start(raw[:, t, :], rows[t])
                 with nc.allow_non_contiguous_dma(reason="one gain value for each partition"):
@@ -247,11 +247,11 @@ def tile_list_sprinkler_layout_review_kernel(
             cols = slice(P * t, P * t + P)
             return first_stage(
                 [(wa_q[a, b][0][:, cols].bitcast(FP8X4), wa_q[a, b][1][:, cols], v1w[a], v1s, ROW1 + 4 * a) for a in range(2)],
-                "rows", 8, "a_win")
+                "rows", RB, "a_win")
 
         def hazard(s, part, parts):
             width = NP // parts
-            f = work.tile([P, width], F32, name="f", tag="tmp", bufs=4)
+            f = work.tile([P, width], F32, name="f", tag="tmp", bufs=TB)
             places = pos1_t[:, part * width // 16 : (part + 1) * width // 16]
             nc.vector.tensor_tensor(f[:], a_win[s][:].indirect(places), usable[s][:, part * width : (part + 1) * width], SUB)
             return f
@@ -263,7 +263,8 @@ def tile_list_sprinkler_layout_review_kernel(
         def weave(rows, name):
             width = rows.shape[2]
             grouped = work.tile([P, 4 * width], BF16, name=name, tag="grouped", bufs=3, align_bytes=64)
-            nc.vector.tensor_copy(grouped[:].rearrange("p (j t) -> p j t", t=4), rows[:].rearrange("p t j -> p j t"))
+            nc.vector.tensor_copy(
+                grouped[:].rearrange("p (c i t) -> p c t i", i=4, t=4), rows[:].rearrange("p t (c i) -> p c t i", i=4))
             return grouped
 
         wo_q = {}

@@ -22,14 +22,14 @@ BANK = 512
 SLICES = H // P
 WINDOW_BYTES = 4 * T
 DB = 3
-BB = 4
+BB = 5
 LAG = 3
 AB = 2
 PARTS = 2
-YB = 3
-TB = 5
-LEAD = 3
-RB = 7
+YB = 4
+TB = 6
+LEAD = 4
+RB = 6
 ROW3 = 4
 ROW1 = 8
 
@@ -95,11 +95,11 @@ def tile_list_sprinkler_layout_review_kernel(
             return work.tile([P, T], U8, name=name, tag="page", bufs=3, align_bytes=64)
 
         sc2_win = scale_window("sc2_win")
-        sc3_win = scale_window("sc3_win")
         sc1_win = scale_window("sc1_win")
+        sc3_win = scale_window("sc3_win")
         w4s_raw = keep.tile([P, H], U8, name="w4s_raw", align_bytes=64)
         w8s_raw = keep.tile([P, H], U8, name="w8s_raw", align_bytes=64)
-        for plane in (sc2_win, sc3_win, sc1_win, w4s_raw, w8s_raw):
+        for plane in (sc2_win, sc1_win, sc3_win, w4s_raw, w8s_raw):
             nc.vector.memset(plane[:].bitcast(I32), 0)
         warm = keep.tile([P, 8], F32, name="warm")
         nc.vector.memset(warm[:], 0.0)
@@ -112,14 +112,15 @@ def tile_list_sprinkler_layout_review_kernel(
         for q in range(4):
             load_scale_rows(sc2_win, tab2_scales, q, 0, nc.sync)
         load_words(tab2_win, tab2_words[0], 0, 2)
+        for q in range(4):
+            load_scale_rows(sc3_win, tab3_scales, q, ROW3, nc.sync)
         load_words(tab2_win, tab2_words[0], 1, 2)
         w4_raw = keep.tile([P, 2 * H], U8, name="w4_raw", align_bytes=64)
         nc.sync.dma_start(w4_raw[:].bitcast(I32), w4_words[0].bitcast(I32))
         for q in range(4):
             load_scale_rows(w4s_raw, w4_scales, q, 0, nc.sync)
         load_words(tab3_win, tab3_words[0], 0, 2)
-        for q in range(4):
-            load_scale_rows(sc3_win, tab3_scales, q, ROW3, nc.sync)
+        offs_t = load_list(offs, "offs_t")
         load_words(tab3_win, tab3_words[0], 1, 2)
         w8_raw = keep.tile([P, 4 * H], U8, name="w8_raw", align_bytes=64)
         nc.sync.dma_start(w8_raw[:].bitcast(I32), w8_words[0].rearrange("p n t -> p (n t)").bitcast(I32))
@@ -127,7 +128,6 @@ def tile_list_sprinkler_layout_review_kernel(
             load_scale_rows(w8s_raw, w8_scales, q, ROW3, nc.sync)
         pos2_t = load_list(pos2, "pos2_t")
         pos3_t = load_list(pos3, "pos3_t")
-        offs_t = load_list(offs, "offs_t")
 
         for q in range(4):
             load_scale_rows(sc1_win, tab_scales, q, ROW1, nc.gpsimd)
@@ -163,9 +163,10 @@ def tile_list_sprinkler_layout_review_kernel(
 
         b_win = {s: stage_b(s) for s in range(BB)}
 
+        v1s = gather_bytes(sc1_win, offs_t, U8, "v1s")
+        v3w = gather_bytes(tab3_win, offs3_t, U32, "v3w")
         w8_d = deal(w8_raw, "w8_d")
         w8s_d = deal(w8s_raw, "w8s_d")
-        v3w = gather_bytes(tab3_win, offs3_t, U32, "v3w")
 
         wa_raw = {}
 
@@ -209,7 +210,6 @@ def tile_list_sprinkler_layout_review_kernel(
         wa_grouped = {}
         v1w = {}
         b_picked = {s: pick_b(s) for s in range(BB)}
-        v1s = gather_bytes(sc1_win, offs_t, U8, "v1s")
         for s in range(SLICES + LAG):
             if s < SLICES:
                 d_win = stage_d(s)

@@ -21,13 +21,13 @@ P = 128
 BANK = 512
 SLICES = H // P
 WINDOW_BYTES = 4 * T
-DB = 3
+DB = 4
 BB = 5
 LAG = 3
 AB = 2
 PARTS = 2
 YB = 4
-TB = 6
+TB = 7
 LEAD = 4
 RB = 6
 ROW3 = 4
@@ -53,8 +53,8 @@ def tile_list_sprinkler_layout_review_kernel(
         def words_window(name, place):
             return arena.tile([P, T], U32, name=name, offset=place * WINDOW_BYTES)
 
-        def load_words(tile, src, part, parts):
-            cols = slice(part * T // parts, (part + 1) * T // parts)
+        def load_words(tile, src, first, last):
+            cols = slice(first * T // 8, last * T // 8)
             nc.sync.dma_start(tile[:, cols].bitcast(I32), src[:, cols, :].rearrange("p n t -> p (n t)").bitcast(I32))
 
         def load_scale_rows(tile, src, q, row, queue):
@@ -108,20 +108,21 @@ def tile_list_sprinkler_layout_review_kernel(
         tab2_win = words_window("tab2_win", 0)
         tab3_win = words_window("tab3_win", 1)
         offs2_t = load_list(offs2, "offs2_t")
-        offs3_t = load_list(offs3, "offs3_t")
-        for q in range(4):
-            load_scale_rows(sc2_win, tab2_scales, q, 0, nc.sync)
-        load_words(tab2_win, tab2_words[0], 0, 2)
-        for q in range(4):
-            load_scale_rows(sc3_win, tab3_scales, q, ROW3, nc.sync)
-        load_words(tab2_win, tab2_words[0], 1, 2)
         w4_raw = keep.tile([P, 2 * H], U8, name="w4_raw", align_bytes=64)
         nc.sync.dma_start(w4_raw[:].bitcast(I32), w4_words[0].bitcast(I32))
         for q in range(4):
+            load_scale_rows(sc2_win, tab2_scales, q, 0, nc.sync)
+        load_words(tab2_win, tab2_words[0], 0, 3)
+        offs3_t = load_list(offs3, "offs3_t")
+        for q in range(4):
+            load_scale_rows(sc3_win, tab3_scales, q, ROW3, nc.sync)
+        load_words(tab2_win, tab2_words[0], 3, 7)
+        for q in range(4):
             load_scale_rows(w4s_raw, w4_scales, q, 0, nc.sync)
-        load_words(tab3_win, tab3_words[0], 0, 2)
+        load_words(tab2_win, tab2_words[0], 7, 8)
+        load_words(tab3_win, tab3_words[0], 0, 4)
         offs_t = load_list(offs, "offs_t")
-        load_words(tab3_win, tab3_words[0], 1, 2)
+        load_words(tab3_win, tab3_words[0], 4, 8)
         w8_raw = keep.tile([P, 4 * H], U8, name="w8_raw", align_bytes=64)
         nc.sync.dma_start(w8_raw[:].bitcast(I32), w8_words[0].rearrange("p n t -> p (n t)").bitcast(I32))
         for q in range(4):
@@ -134,34 +135,51 @@ def tile_list_sprinkler_layout_review_kernel(
 
         v2s = gather_bytes(sc2_win, offs2_t, U8, "v2s")
         v3s = gather_bytes(sc3_win, offs3_t, U8, "v3s")
-        v2w = gather_bytes(tab2_win, offs2_t, U32, "v2w")
         w4_d = deal(w4_raw, "w4_d")
         w4s_d = deal(w4s_raw, "w4s_d")
+        v2w = keep.tile([P, S], U32, name="v2w", align_bytes=64)
+        for h in range(2):
+            nc.vector.tensor_copy(v2w[:, h * BANK : (h + 1) * BANK], tab2_win[:].indirect(offs2_t[:, 32 * h : 32 * h + 32]))
 
-        def first_stage(passes, tag, bufs, name):
-            window = work.tile([P, S], F32, name=name, tag=tag, bufs=bufs)
-            for h in range(S // BANK):
-                cols = slice(h * BANK, (h + 1) * BANK)
-                acc = psum.tile([P, BANK], F32, name="acc", tag="acc")
-                for n, (lw, ls, rw, rs, row) in enumerate(passes):
-                    nc.tensor.matmul_mx(
-                        out=acc[:], lhsT=lw, lhsT_scale=ls, rhs=rw[:, cols].bitcast(FP8X4), rhs_scale=rs[row:P, cols],
-                        start=(n == 0), stop=(n == len(passes) - 1),
-                    )
+        def rows_tile(tag, bufs, name):
+            return work.tile([P, S], F32, name=name, tag=tag, bufs=bufs)
+
+        def fill_half(window, h, passes, negate=False):
+            cols = slice(h * BANK, (h + 1) * BANK)
+            acc = psum.tile([P, BANK], F32, name="acc", tag="acc")
+            for n, (lw, ls, rw, rs, row) in enumerate(passes):
+                nc.tensor.matmul_mx(
+                    out=acc[:], lhsT=lw, lhsT_scale=ls, rhs=rw[:, cols].bitcast(FP8X4), rhs_scale=rs[row:P, cols],
+                    start=(n == 0), stop=(n == len(passes) - 1),
+                )
+            if negate:
+                nc.scalar.activation(window[:, cols], acc[:], COPY, scale=-1.0)
+            else:
                 nc.scalar.copy(window[:, cols], acc[:])
+
+        def first_stage(passes, tag, bufs, name, negate=False):
+            window = rows_tile(tag, bufs, name)
+            for h in range(S // BANK):
+                fill_half(window, h, passes, negate)
             return window
 
+        def passes_b(s):
+            return [(w4_d[:, 256 * s : 256 * s + 256].bitcast(FP4X4), w4s_d[:, P * s : P * s + P], v2w, v2s, 0)]
+
         def stage_b(s):
-            return first_stage(
-                [(w4_d[:, 256 * s : 256 * s + 256].bitcast(FP4X4), w4s_d[:, P * s : P * s + P], v2w, v2s, 0)],
-                "rows", RB, "b_win")
+            return first_stage(passes_b(s), "rows", RB, "b_win")
 
         def stage_d(s):
             return first_stage(
                 [(w8_d[:, 512 * s : 512 * s + 512].bitcast(FP8X4), w8s_d[ROW3:P, P * s : P * s + P], v3w, v3s, ROW3)],
                 "d_rows", DB, "d_win")
 
-        b_win = {s: stage_b(s) for s in range(BB)}
+        b_win = {s: rows_tile("rows", RB, "b_win") for s in range(2)}
+        for h in range(2):
+            for s in range(2):
+                fill_half(b_win[s], h, passes_b(s))
+        for s in range(2, BB):
+            b_win[s] = stage_b(s)
 
         v1s = gather_bytes(sc1_win, offs_t, U8, "v1s")
         v3w = gather_bytes(tab3_win, offs3_t, U32, "v3w")
@@ -182,13 +200,13 @@ def tile_list_sprinkler_layout_review_kernel(
 
         tab_win = [words_window("tab_win%d" % a, 2 + a) for a in range(2)]
         for a in range(2):
-            load_words(tab_win[a], tab_words[a], 0, 1)
+            load_words(tab_win[a], tab_words[a], 0, 8)
         load_wa(1)
         pos1_t = load_list(pos1, "pos1_t")
 
         def cast_wa(a, b):
             grouped = grouped_tile("wa_grouped")
-            cast(True,
+            cast(2 * b + a not in (3,),
                  grouped[:].rearrange("p (t u i j) -> p u t j i", t=4, i=4, j=4),
                  wa_raw[a, b][:].rearrange("p j (u t i) -> p u t j i", t=4, i=4))
             return grouped
@@ -260,11 +278,11 @@ def tile_list_sprinkler_layout_review_kernel(
             nc.scalar.activation(f[:], f[:], SILU)
             nc.scalar.activation(z_rows[:, s % 4, :], f[:], COPY, scale=gain_t[:, s, 0:1])
 
-        def weave(rows, name):
+        def weave(rows, name, on_scalar=False):
             width = rows.shape[2]
             grouped = work.tile([P, 4 * width], BF16, name=name, tag="grouped", bufs=3, align_bytes=64)
-            nc.vector.tensor_copy(
-                grouped[:].rearrange("p (c i t) -> p c t i", i=4, t=4), rows[:].rearrange("p t (c i) -> p c t i", i=4))
+            cast(on_scalar,
+                 grouped[:].rearrange("p (c i t) -> p c t i", i=4, t=4), rows[:].rearrange("p t (c i) -> p c t i", i=4))
             return grouped
 
         wo_q = {}
@@ -276,13 +294,12 @@ def tile_list_sprinkler_layout_review_kernel(
             for n in range(AB + 2 * s, min(SLICES, AB + 2 * s + 2)):
                 a_win[n] = stage_a(n)
             piece = divmod(s, 2)
-            wo_grouped[piece] = cast_wo(piece[0], piece[1], s in (0,))
+            wo_grouped[piece] = cast_wo(piece[0], piece[1], s in (3,))
             gained(s, f, z_rows)
             wo_q[piece] = quantize(wo_grouped[piece], "wo%d%d" % piece)
-        z0_grouped = weave(z_rows, "z_grouped")
+        z0_grouped = weave(z_rows, "z_grouped", False)
 
         y_scales = keep.tile([P, 2, NP], U8, name="y_scales", align_bytes=64)
-        y_codes = [keep.tile([P, NP], U32, name="y_codes%d" % g, align_bytes=64) for g in range(2)]
         z1_codes = keep.tile([P, NP], U32, name="z1_codes", align_bytes=64)
         z1_scales = keep.tile([P, NP], U8, name="z1_scales", align_bytes=64)
         width = NP // PARTS
@@ -295,12 +312,12 @@ def tile_list_sprinkler_layout_review_kernel(
 
         def last_stage(part, rows):
             js = slice(part * width, (part + 1) * width)
-            grouped = weave(rows, "z_grouped")
+            grouped = weave(rows, "z_grouped", part in (-1,))
             nc.vector.quantize_mx(out=z1_codes[:, js].bitcast(FP8X4), scales=z1_scales[:, js], in_=grouped[:])
             z_q = [z0_q, (z1_codes, z1_scales)]
             y_rows = []
             for g in range(2):
-                rows = work.tile([P, 4, width], F32, name="y_rows", tag="y_rows", bufs=YB)
+                rows = arena.tile([P, 4, width], F32, name="y_rows%d%d" % (part, g), offset=(2 * part + g) * 16 * width)
                 for t in range(4):
                     cols = slice(P * t, P * t + P)
                     acc = psum.tile([P, width], F32, name="acc", tag="acc")
@@ -316,11 +333,12 @@ def tile_list_sprinkler_layout_review_kernel(
 
         def planes(part, y_rows):
             js = slice(part * width, (part + 1) * width)
+            y_codes = keep.tile([P, 2, width], U32, name="y_codes%d" % part, align_bytes=64)
             for g in range(2):
-                grouped = weave(y_rows[g], "y_grouped")
-                nc.vector.quantize_mx(out=y_codes[g][:, js].bitcast(FP8X4), scales=y_scales[:, g, js], in_=grouped[:])
-                nc.sync.dma_start(
-                    out_1[g][:, js, :].rearrange("p m t -> p (m t)").bitcast(I32), y_codes[g][:, js].bitcast(I32))
+                grouped = weave(y_rows[g], "y_grouped", 2 * part + g in (-1,))
+                nc.vector.quantize_mx(out=y_codes[:, g, :].bitcast(FP8X4), scales=y_scales[:, g, js], in_=grouped[:])
+            nc.sync.dma_start(
+                out_1[:, :, js, :].rearrange("g p m t -> p g (m t)").bitcast(I32), y_codes[:].bitcast(I32))
 
         z1_rows = {0: make_z1(0)}
         z0_q = quantize(z0_grouped, "z0")

from contextlib import ExitStack

import concourse.mybir as mybir

T, S, NP, K, K2, H, N = 4096, 1024, 512, 1024, 512, 1024, 1024
FLOPS = 2 * (K * H * S + 2 * K2 * H * S + H * N * NP)

F32 = mybir.dt.float32
BF16 = mybir.dt.bfloat16
I32 = mybir.dt.int32
U32 = mybir.dt.uint32
U16 = mybir.dt.uint16
U8 = mybir.dt.uint8
FP8X4 = mybir.dt.float8_e4m3fn_x4
FP4X4 = mybir.dt.float4_e2m1fn_x4
SILU = mybir.ActivationFunctionType.Silu
COPY = mybir.ActivationFunctionType.Copy
SUB = mybir.AluOpType.subtract

P = 128
BANK = 512
SLICES = H // P
WINDOW_BYTES = 4 * T
DB = 4
BB = 5
LAG = 3
AB = 2
PARTS = 2
YB = 4
TB = 7
LEAD = 4
RB = 6
ROW3 = 4
ROW1 = 8


def tile_list_sprinkler_layout_review_kernel(
    tc, tab_words, tab_scales, tab2_words, tab2_scales, tab3_words, tab3_scales, offs, offs2, offs3,
    pos1, pos2, pos3, wa, w4_words, w4_scales, w8_words, w8_scales, gain, wo, out_0, out_1, out_2,
):
    nc = tc.nc
    with ExitStack() as ctx:
        keep = ctx.enter_context(tc.tile_pool(name="keep", bufs=1))
        work = ctx.enter_context(tc.tile_pool(name="work", bufs=1))
        arena = ctx.enter_context(tc.tile_pool(name="arena", bufs=1))
        psum = ctx.enter_context(tc.psum_pool(name="psum", bufs=8))

        def load_list(src, name):
            tile = keep.tile([P, src.shape[1]], U16, name=name)
            nc.sync.dma_start(tile[:], src)
            return tile

        def words_window(name, place):
            return arena.tile([P, T], U32, name=name, offset=place * WINDOW_BYTES)

        def load_words(tile, src, first, last):
            cols = slice(first * T // 8, last * T // 8)
            nc.sync.dma_start(tile[:, cols].bitcast(I32), src[:, cols, :].rearrange("p n t -> p (n t)").bitcast(I32))

        def load_scale_rows(tile, src, q, row, queue):
            passes = src.shape[0]
            rows = src[:, 4 * q : 4 * q + 4, :] if passes > 1 else src[0, 4 * q : 4 * q + 4, :]
            queue.dma_start(tile[32 * q + row : 32 * q + row + 4 * passes, :].bitcast(I32), rows.bitcast(I32))

        def gather_bytes(window, offsets, dtype, name):
            tile = keep.tile([P, S], dtype, name=name, align_bytes=64)
            nc.vector.tensor_copy(tile[:], window[:].indirect(offsets[:]))
            return tile

        def deal(raw, name):
            width = raw.shape[1]
            tile = keep.tile([P, width], U8, name=name, align_bytes=64)
            nc.vector.tensor_copy(
                tile[:].bitcast(I32).rearrange("p (b t u i) -> p b u t i", b=2, t=4, u=32),
                raw[:].bitcast(I32).rearrange("p (b u t i) -> p b u t i", b=2, t=4, u=32),
            )
            return tile

        def quantize(grouped, name):
            codes = keep.tile([P, BANK], U32, name=name + "_codes", align_bytes=64)
            scales = keep.tile([P, BANK], U8, name=name + "_scales", align_bytes=64)
            nc.vector.quantize_mx(out=codes[:].bitcast(FP8X4), scales=scales[:], in_=grouped[:])
            return codes, scales

        def grouped_tile(name):
            return work.tile([P, 4 * BANK], BF16, name=name, tag="grouped", bufs=3, align_bytes=64)

        def cast(on_scalar, out, in_):
            if on_scalar:
                nc.scalar.copy(out, in_)
            else:
                nc.vector.tensor_copy(out, in_)

        def scale_window(name):
            return work.tile([P, T], U8, name=name, tag="page", bufs=3, align_bytes=64)

        sc2_win = scale_window("sc2_win")
        sc1_win = scale_window("sc1_win")
        sc3_win = scale_window("sc3_win")
        w4s_raw = keep.tile([P, H], U8, name="w4s_raw", align_bytes=64)
        w8s_raw = keep.tile([P, H], U8, name="w8s_raw", align_bytes=64)
        for plane in (sc2_win, sc1_win, sc3_win, w4s_raw, w8s_raw):
            nc.vector.memset(plane[:].bitcast(I32), 0)
        warm = keep.tile([P, 8], F32, name="warm")
        nc.vector.memset(warm[:], 0.0)
        nc.scalar.activation(warm[:, 1:2], warm[:, 0:1], SILU)

        tab2_win = words_window("tab2_win", 0)
        tab3_win = words_window("tab3_win", 1)
        offs2_t = load_list(offs2, "offs2_t")
        w4_raw = keep.tile([P, 2 * H], U8, name="w4_raw", align_bytes=64)
        nc.sync.dma_start(w4_raw[:].bitcast(I32), w4_words[0].bitcast(I32))
        for q in range(4):
            load_scale_rows(sc2_win, tab2_scales, q, 0, nc.sync)
        load_words(tab2_win, tab2_words[0], 0, 3)
        offs3_t = load_list(offs3, "offs3_t")
        for q in range(4):
            load_scale_rows(sc3_win, tab3_scales, q, ROW3, nc.sync)
        load_words(tab2_win, tab2_words[0], 3, 7)
        for q in range(4):
            load_scale_rows(w4s_raw, w4_scales, q, 0, nc.sync)
        load_words(tab2_win, tab2_words[0], 7, 8)
        load_words(tab3_win, tab3_words[0], 0, 4)
        offs_t = load_list(offs, "offs_t")
        load_words(tab3_win, tab3_words[0], 4, 8)
        w8_raw = keep.tile([P, 4 * H], U8, name="w8_raw", align_bytes=64)
        nc.sync.dma_start(w8_raw[:].bitcast(I32), w8_words[0].rearrange("p n t -> p (n t)").bitcast(I32))
        for q in range(4):
            load_scale_rows(w8s_raw, w8_scales, q, ROW3, nc.sync)
        pos2_t = load_list(pos2, "pos2_t")
        pos3_t = load_list(pos3, "pos3_t")

        for q in range(4):
            load_scale_rows(sc1_win, tab_scales, q, ROW1, nc.gpsimd)

        v2s = gather_bytes(sc2_win, offs2_t, U8, "v2s")
        v3s = gather_bytes(sc3_win, offs3_t, U8, "v3s")
        w4_d = deal(w4_raw, "w4_d")
        w4s_d = deal(w4s_raw, "w4s_d")
        v2w = keep.tile([P, S], U32, name="v2w", align_bytes=64)
        for h in range(2):
            nc.vector.tensor_copy(v2w[:, h * BANK : (h + 1) * BANK], tab2_win[:].indirect(offs2_t[:, 32 * h : 32 * h + 32]))

        def rows_tile(tag, bufs, name):
            return work.tile([P, S], F32, name=name, tag=tag, bufs=bufs)

        def fill_half(window, h, passes, negate=False):
            cols = slice(h * BANK, (h + 1) * BANK)
            acc = psum.tile([P, BANK], F32, name="acc", tag="acc")
            for n, (lw, ls, rw, rs, row) in enumerate(passes):
                nc.tensor.matmul_mx(
                    out=acc[:], lhsT=lw, lhsT_scale=ls, rhs=rw[:, cols].bitcast(FP8X4), rhs_scale=rs[row:P, cols],
                    start=(n == 0), stop=(n == len(passes) - 1),
                )
            if negate:
                nc.scalar.activation(window[:, cols], acc[:], COPY, scale=-1.0)
            else:
                nc.scalar.copy(window[:, cols], acc[:])

        def first_stage(passes, tag, bufs, name, negate=False):
            window = rows_tile(tag, bufs, name)
            for h in range(S // BANK):
                fill_half(window, h, passes, negate)
            return window

        def passes_b(s):
            return [(w4_d[:, 256 * s : 256 * s + 256].bitcast(FP4X4), w4s_d[:, P * s : P * s + P], v2w, v2s, 0)]

        def stage_b(s):
            return first_stage(passes_b(s), "rows", RB, "b_win")

        def stage_d(s):
            return first_stage(
                [(w8_d[:, 512 * s : 512 * s + 512].bitcast(FP8X4), w8s_d[ROW3:P, P * s : P * s + P], v3w, v3s, ROW3)],
                "d_rows", DB, "d_win")

        b_win = {s: rows_tile("rows", RB, "b_win") for s in range(2)}
        for h in range(2):
            for s in range(2):
                fill_half(b_win[s], h, passes_b(s))
        for s in range(2, BB):
            b_win[s] = stage_b(s)

        v1s = gather_bytes(sc1_win, offs_t, U8, "v1s")
        v3w = gather_bytes(tab3_win, offs3_t, U32, "v3w")
        w8_d = deal(w8_raw, "w8_d")
        w8s_d = deal(w8s_raw, "w8s_d")

        wa_raw = {}

        def load_wa(b):
            for a in range(2):
                raw = arena.tile([P, 4, BANK], F32, name="wa_raw%d%d" % (a, b), offset=(2 * b + a) * WINDOW_BYTES // 2)
                nc.sync.dma_start(
                    raw[:], wa[512 * a : 512 * a + 512, 512 * b : 512 * b + 512].rearrange("(p j) c -> p j c", j=4)
                )
                wa_raw[a, b] = raw

        load_wa(0)

        tab_win = [words_window("tab_win%d" % a, 2 + a) for a in range(2)]
        for a in range(2):
            load_words(tab_win[a], tab_words[a], 0, 8)
        load_wa(1)
        pos1_t = load_list(pos1, "pos1_t")

        def cast_wa(a, b):
            grouped = grouped_tile("wa_grouped")
            cast(2 * b + a not in (3,),
                 grouped[:].rearrange("p (t u i j) -> p u t j i", t=4, i=4, j=4),
                 wa_raw[a, b][:].rearrange("p j (u t i) -> p u t j i", t=4, i=4))
            return grouped

        def cast_wo(b, g, on_scalar):
            grouped = grouped_tile("wo_grouped")
            cast(on_scalar,
                 grouped[:].rearrange("p (t m j) -> p m j t", t=4, j=4),
                 wo_raw[b][:, :, 512 * g : 512 * g + 512].rearrange("p j (m t) -> p m j t", t=4))
            return grouped

        def pick_b(s):
            picked = work.tile([P, NP], F32, name="b_picked", tag="tmp", bufs=TB)
            nc.vector.tensor_copy(picked[:], b_win[s][:].indirect(pos2_t[:]))
            return picked

        usable = {}
        wa_q = {}
        wa_grouped = {}
        v1w = {}
        b_picked = {s: pick_b(s) for s in range(BB)}
        for s in range(SLICES + LAG):
            if s < SLICES:
                d_win = stage_d(s)
                usable[s] = keep.tile([P, NP], F32, name="usable%d" % s)
                nc.vector.tensor_tensor(usable[s][:], d_win[:].indirect(pos3_t[:]), b_picked[s][:], SUB)
            if BB <= s + LEAD < SLICES:
                b_win[s + LEAD] = stage_b(s + LEAD)
                b_picked[s + LEAD] = pick_b(s + LEAD)
            if s < SLICES:
                piece = (s // 2 % 2, s // 4)
                if s % 2 == 0:
                    wa_grouped[piece] = cast_wa(*piece)
                else:
                    wa_q[piece] = quantize(wa_grouped[piece], "wa%d%d" % piece)
            if s >= LAG:
                nc.scalar.activation(usable[s - LAG][:], usable[s - LAG][:], SILU, scale=-1.0)
            if s in (4, 6):
                a = len(v1w)
                v1w[a] = gather_bytes(tab_win[a], offs_t, U32, "v1w%d" % a)

        wo_raw = []
        gain_t = keep.tile([P, SLICES, 8], F32, name="gain_t")
        gain_v = gain.rearrange("(b u t i o) -> b t u i o", b=2, u=32, t=4, i=4)
        for b in range(2):
            raw = arena.tile([P, 4, N], F32, name="wo_raw%d" % b, offset=(2 + b) * WINDOW_BYTES)
            rows = wo[512 * b : 512 * b + 512, :].rearrange("(u t i) n -> t u i n", t=4, i=4)
            for t in range(4):
                nc.sync.dma_start(raw[:, t, :], rows[t])
                with nc.allow_non_contiguous_dma(reason="one gain value for each partition"):
                    nc.sync.dma_start(gain_t[:, 4 * b + t, 0:1], gain_v[b, t])
            wo_raw.append(raw)

        def stage_a(s):
            b, t = divmod(s, 4)
            cols = slice(P * t, P * t + P)
            return first_stage(
                [(wa_q[a, b][0][:, cols].bitcast(FP8X4), wa_q[a, b][1][:, cols], v1w[a], v1s, ROW1 + 4 * a) for a in range(2)],
                "rows", RB, "a_win")

        def hazard(s, part, parts):
            width = NP // parts
            f = work.tile([P, width], F32, name="f", tag="tmp", bufs=TB)
            places = pos1_t[:, part * width // 16 : (part + 1) * width // 16]
            nc.vector.tensor_tensor(f[:], a_win[s][:].indirect(places), usable[s][:, part * width : (part + 1) * width], SUB)
            return f

        def gained(s, f, z_rows):
            nc.scalar.activation(f[:], f[:], SILU)
            nc.scalar.activation(z_rows[:, s % 4, :], f[:], COPY, scale=gain_t[:, s, 0:1])

        def weave(rows, name, on_scalar=False):
            width = rows.shape[2]
            grouped = work.tile([P, 4 * width], BF16, name=name, tag="grouped", bufs=3, align_bytes=64)
            cast(on_scalar,
                 grouped[:].rearrange("p (c i t) -> p c t i", i=4, t=4), rows[:].rearrange("p t (c i) -> p c t i", i=4))
            return grouped

        wo_q = {}
        wo_grouped = {}
        a_win = {s: stage_a(s) for s in range(AB)}
        z_rows = work.tile([P, 4, NP], BF16, name="z_rows", tag="page", bufs=3, align_bytes=64)
        for s in range(4):
            f = hazard(s, 0, 1)
            for n in range(AB + 2 * s, min(SLICES, AB + 2 * s + 2)):
                a_win[n] = stage_a(n)
            piece = divmod(s, 2)
            wo_grouped[piece] = cast_wo(piece[0], piece[1], s in (3,))
            gained(s, f, z_rows)
            wo_q[piece] = quantize(wo_grouped[piece], "wo%d%d" % piece)
        z0_grouped = weave(z_rows, "z_grouped", False)

        y_scales = keep.tile([P, 2, NP], U8, name="y_scales", align_bytes=64)
        z1_codes = keep.tile([P, NP], U32, name="z1_codes", align_bytes=64)
        z1_scales = keep.tile([P, NP], U8, name="z1_scales", align_bytes=64)
        width = NP // PARTS

        def make_z1(part):
            rows = work.tile([P, 4, width], BF16, name="z1_rows", tag="page", bufs=3, align_bytes=64)
            for s in range(4, SLICES):
                gained(s, hazard(s, part, PARTS), rows)
            return rows

        def last_stage(part, rows):
            js = slice(part * width, (part + 1) * width)
            grouped = weave(rows, "z_grouped", part in (-1,))
            nc.vector.quantize_mx(out=z1_codes[:, js].bitcast(FP8X4), scales=z1_scales[:, js], in_=grouped[:])
            z_q = [z0_q, (z1_codes, z1_scales)]
            y_rows = []
            for g in range(2):
                rows = arena.tile([P, 4, width], F32, name="y_rows%d%d" % (part, g), offset=(2 * part + g) * 16 * width)
                for t in range(4):
                    cols = slice(P * t, P * t + P)
                    acc = psum.tile([P, width], F32, name="acc", tag="acc")
                    for b in range(2):
                        nc.tensor.matmul_mx(
                            out=acc[:], lhsT=wo_q[b, g][0][:, cols].bitcast(FP8X4), lhsT_scale=wo_q[b, g][1][:, cols],
                            rhs=z_q[b][0][:, js].bitcast(FP8X4), rhs_scale=z_q[b][1][:, js], start=(b == 0), stop=(b == 1),
                        )
                    nc.scalar.copy(rows[:, t, :], acc[:])
                nc.sync.dma_start(out_0[512 * g : 512 * g + 512, js].rearrange("(p t) j -> p t j", t=4), rows[:])
                y_rows.append(rows)
            return y_rows

        def planes(part, y_rows):
            js = slice(part * width, (part + 1) * width)
            y_codes = keep.tile([P, 2, width], U32, name="y_codes%d" % part, align_bytes=64)
            for g in range(2):
                grouped = weave(y_rows[g], "y_grouped", 2 * part + g in (-1,))
                nc.vector.quantize_mx(out=y_codes[:, g, :].bitcast(FP8X4), scales=y_scales[:, g, js], in_=grouped[:])
            nc.sync.dma_start(
                out_1[:, :, js, :].rearrange("g p m t -> p g (m t)").bitcast(I32), y_codes[:].bitcast(I32))

        z1_rows = {0: make_z1(0)}
        z0_q = quantize(z0_grouped, "z0")
        y_rows = {}
        for part in range(PARTS):
            if part + 1 < PARTS:
                z1_rows[part + 1] = make_z1(part + 1)
            y_rows[part] = last_stage(part, z1_rows[part])
            if part > 0:
                planes(part - 1, y_rows[part - 1])
        planes(PARTS - 1, y_rows[PARTS - 1])
        for q in range(4):
            nc.sync.dma_start(
                out_2[:, 4 * q : 4 * q + 4, :].rearrange("g q m -> q g m").bitcast(I32),
                y_scales[32 * q : 32 * q + 4, :, :].bitcast(I32),
            )
